import numpy as np
import ml_dtypes


def mxq(x, axis, fmt="e4m3"):
    dtype, down = {"e4m3": (ml_dtypes.float8_e4m3fn, 7), "e5m2": (ml_dtypes.float8_e5m2, 14)}[fmt]
    v = np.moveaxis(np.asarray(x, np.float32).astype(ml_dtypes.bfloat16).astype(np.float64), axis, -1)
    blocks = v.reshape(v.shape[:-1] + (-1, 32))
    amax = np.abs(blocks).max(-1, keepdims=True)
    byte = np.maximum(np.where(amax > 0, np.frexp(amax)[1] - 1 + 127, 0) - down, 1)
    scale = np.exp2(byte - 127.0)
    codes = (blocks / scale).astype(np.float32).astype(dtype).astype(np.float64)
    return np.moveaxis((codes * scale).reshape(v.shape), -1, axis)


WIDE = False


def mx_kscale(k):
    if not WIDE:
        return np.ones(k)
    levels = np.array([10, -10, 5, -5, 0])
    if k % 512:
        return np.exp2(np.random.permutation(np.resize(levels, k // 32))).repeat(32)
    a = np.empty((k // 512, 16))
    for p in range(k // 512):
        a[p, :8] = np.random.permutation(np.resize(levels, 8))
        for g in range(8):
            far = levels[np.abs(levels - a[p, g]) >= 10]
            a[p, g + 8] = far[np.random.randint(len(far))]
    return np.exp2(a.ravel()).repeat(32)


def f64(x):
    return np.asarray(x).astype(np.float64)


def striped(idx):
    return np.tile(idx.reshape(-1, 16).T, (8, 1)).astype(np.uint16)


def unstriped(offs):
    return offs[:16].T.reshape(-1).astype(np.int64)


E2M1 = np.array([0.0, 0.5, 1.0, 1.5, 2.0, 3.0, 4.0, 6.0, -0.0, -0.5, -1.0, -1.5, -2.0, -3.0, -4.0, -6.0])


def pack_weight(w, fmt):
    k, n = w.shape
    w = f64(np.asarray(w, np.float32).astype(ml_dtypes.bfloat16)).reshape(k // 32, 32, n)
    amax = np.abs(w).max(1)
    if fmt == "e4m3":
        byte = np.frexp(amax)[1] - 1 + 127 - 7
    else:
        mant, ex = np.frexp(amax / 6.0)
        byte = np.where(mant > 0.5, ex, ex - 1) + 127
    byte = np.clip(np.where(amax > 0, byte, 1), 1, 254)
    scaled = (w * np.exp2(127.0 - byte)[:, None, :]).reshape(k, n).astype(np.float32)
    by_word = np.ascontiguousarray(scaled.reshape(k // 512, 128, 4, n).transpose(0, 1, 3, 2))
    if fmt == "e4m3":
        words = by_word.astype(ml_dtypes.float8_e4m3fn).view(np.uint8)
    else:
        c = by_word.astype(ml_dtypes.float4_e2m1fn).view(np.uint8) & 0xF
        words = (c[..., 0::2] | (c[..., 1::2] << 4)).reshape(k // 512, 128, 2 * n)
    return np.ascontiguousarray(words), np.ascontiguousarray(byte.astype(np.uint8).reshape(k // 512, 16, n))


def unpack_weight(words, scales, fmt):
    g, _, n = scales.shape
    words = np.ascontiguousarray(words).reshape(g, 128, n, -1)
    if fmt == "e4m3":
        vals = words.view(ml_dtypes.float8_e4m3fn).astype(np.float64)
    else:
        nib = np.empty((g, 128, n, 4), np.uint8)
        nib[..., 0::2] = words & 0xF
        nib[..., 1::2] = words >> 4
        vals = E2M1[nib]
    vals = vals * np.repeat(np.exp2(scales.astype(np.float64) - 127.0), 8, axis=1)[..., None]
    return vals.transpose(0, 1, 3, 2).reshape(g * 512, n)


def gelu(v):
    return 0.5 * v * (1.0 + np.tanh(np.sqrt(2.0 / np.pi) * (v + 0.044715 * v**3)))


K, K2, H, N, T, S = 1024, 512, 1024, 384, 4096, 1024


def setup_inputs():
    n = np.random.standard_normal
    s = mx_kscale(K)[:, None]
    s2 = mx_kscale(K2)[:, None]
    u = mx_kscale(H)[:, None]
    d = {}
    d["tab_words"], d["tab_scales"] = pack_weight(n((K, T)) * s, "e4m3")
    d["offs"] = striped(np.random.permutation(T)[:S])
    d["xs_words"], d["xs_scales"] = pack_weight(n((K2, S)) * s2, "e4m3")
    d["w1"] = (1.5 * n((K, H)) / K ** 0.5 / s).astype(np.float32)
    d["wx_words"], d["wx_scales"] = pack_weight(n((K2, H)) / K2 ** 0.5 / s2, "e2m1")
    d["b1"] = (0.7 * n(H)).astype(np.float32)
    d["gain"] = (np.exp(0.3 * n(H)) * u[:, 0]).astype(np.float32)
    d["w3"] = (n((H, N)) / H ** 0.5 / u).astype(np.float32)
    return d


def reference(tab_words, tab_scales, offs, xs_words, xs_scales, w1, wx_words, wx_scales, b1, gain, w3):
    v = unpack_weight(tab_words, tab_scales, "e4m3")[:, unstriped(offs)]
    xs = unpack_weight(xs_words, xs_scales, "e4m3")
    wx = unpack_weight(wx_words, wx_scales, "e2m1")
    prof = mxq(f64(w1), 0, "e4m3").T @ v
    beam = wx.T @ xs
    dep = prof - beam + f64(b1)[:, None]
    root = np.sqrt(1.0 + np.square(dep))
    h = (root + beam) * f64(gain)[:, None]
    out = mxq(f64(w3), 0, "e4m3").T @ mxq(h, 0, "e4m3")
    return out

@@ -1,0 +1,304 @@
+from contextlib import ExitStack
+
+import concourse.mybir as mybir
+
+K, K2, H, N, T, S = 1024, 512, 1024, 384, 4096, 1024
+FLOPS = 2 * (K * H * S + K2 * H * S + H * N * S)
+
+F32 = mybir.dt.float32
+BF16 = mybir.dt.bfloat16
+I32 = mybir.dt.int32
+U32 = mybir.dt.uint32
+U16 = mybir.dt.uint16
+U8 = mybir.dt.uint8
+FP8X4 = mybir.dt.float8_e4m3fn_x4
+FP4X4 = mybir.dt.float4_e2m1fn_x4
+ALU = mybir.AluOpType
+ACT = mybir.ActivationFunctionType
+
+P = 128
+PACK = 4
+KP = P * PACK
+JC = 512
+TINY = 2.0 ** -120
+REPEATS = 6
+
+
+def tile_list_toll_axle_scores_kernel(
+    tc, tab_words, tab_scales, offs, xs_words, xs_scales, w1, wx_words, wx_scales, b1, gain, w3, out
+):
+    nc = tc.nc
+    with ExitStack() as ctx:
+        keep = ctx.enter_context(tc.tile_pool(name="keep", bufs=1))
+        work = ctx.enter_context(tc.tile_pool(name="work", bufs=4))
+        psum = ctx.enter_context(tc.psum_pool(name="psum", bufs=1))
+
+        def held(name, shape, dtype):
+            return keep.tile(shape, dtype, name=name, align_bytes=64)
+
+        offsets = keep.tile([P, S // 16], U16, name="offsets")
+        wx_raw = held("wx_raw", [P, H // 2], I32)
+        wx_plane_raw = held("wx_plane_raw", [P, H // 4], I32)
+        xs_codes = held("xs_codes", [P, S], I32)
+        xs_plane = held("xs_plane", [P, S // 4], I32)
+        tab_planes = held("tab_planes", [P, T // 4], I32)
+        tab = [held("tab%d" % a, [P, T], I32) for a in range(2)]
+        gains = held("gains", [P, 2, PACK], F32)
+        biases = held("biases", [P, 2, PACK], F32)
+        warm = held("warm", [P, 1], F32)
+        warm_out = held("warm_out", [P, 1], F32)
+
+        nc.vector.memset(wx_plane_raw[:], 0)
+        nc.vector.memset(xs_plane[:], 0)
+        nc.vector.memset(tab_planes[:], 0)
+        nc.vector.memset(warm[:], 1.0)
+        nc.scalar.activation(warm_out[:], warm[:], ACT.Sqrt)
+
+        def load_w1(a, b, c0, c1, name):
+            raw = held(name, [P, PACK, c1 - c0], F32)
+            rows = w1[a * KP : (a + 1) * KP, b * KP + c0 : b * KP + c1]
+            nc.sync.dma_start(raw[:], rows.rearrange("(p i) c -> p i c", i=PACK))
+            return raw
+
+        def load_w3(a):
+            raw = held("w3_raw%d" % a, [P, PACK, N], F32)
+            nc.sync.dma_start(raw[:], w3[a * KP : (a + 1) * KP, :].rearrange("(p i) n -> p i n", i=PACK))
+            return raw
+
+        nc.sync.dma_start(wx_raw[:], wx_words[0].bitcast(I32))
+        for q in range(4):
+            nc.sync.dma_start(wx_plane_raw[32 * q : 32 * q + 4, :], wx_scales[0, 4 * q : 4 * q + 4, :].bitcast(I32))
+        w1_00 = load_w1(0, 0, 0, KP, "w1_00")
+        nc.sync.dma_start(xs_codes[:], xs_words[0].rearrange("p n t -> p (n t)").bitcast(I32))
+        nc.sync.dma_start(gains[:], gain.rearrange("(b p t) -> p b t", b=2, t=PACK))
+        for q in range(4):
+            nc.sync.dma_start(xs_plane[32 * q : 32 * q + 4, :], xs_scales[0, 4 * q : 4 * q + 4, :].bitcast(I32))
+        nc.sync.dma_start(offsets[:], offs)
+        nc.sync.dma_start(tab[0][:], tab_words[0].rearrange("p n t -> p (n t)").bitcast(I32))
+        for q in range(4):
+            nc.sync.dma_start(
+                tab_planes[32 * q : 32 * q + 8, :],
+                tab_scales[:, 4 * q : 4 * q + 4, :].bitcast(I32),
+            )
+        nc.sync.dma_start(tab[1][:], tab_words[1].rearrange("p n t -> p (n t)").bitcast(I32))
+        nc.sync.dma_start(biases[:], b1.rearrange("(b p t) -> p b t", b=2, t=PACK))
+        w1_10a = load_w1(1, 0, 0, KP // 2, "w1_10a")
+        w1_10b = load_w1(1, 0, KP // 2, KP, "w1_10b")
+        w1_01 = load_w1(0, 1, 0, KP, "w1_01")
+        w1_11 = load_w1(1, 1, 0, KP, "w1_11")
+        w3_raw = [load_w3(a) for a in range(2)]
+
+        flat_gains = gains[:].rearrange("p b t -> p (b t)")
+        neg_gains = held("neg_gains", [P, 8], F32)
+        abs_gains = held("abs_gains", [P, 8], F32)
+        denom = held("denom", [P, 8], F32)
+        inv_gains = held("inv_gains", [P, 8], F32)
+        nc.vector.tensor_scalar(neg_gains[:], flat_gains, -1.0, None, ALU.mult)
+        nc.vector.tensor_tensor(abs_gains[:], neg_gains[:], flat_gains, ALU.max)
+        nc.vector.scalar_tensor_tensor(denom[:], abs_gains[:], TINY, flat_gains, ALU.is_lt, ALU.add)
+        nc.vector.reciprocal(inv_gains[:], denom[:])
+
+        wx_codes = held("wx_codes", [P, 2 * H], U8)
+        wx_plane = held("wx_plane", [P, H], U8)
+        nc.vector.tensor_copy(
+            wx_codes[:].bitcast(U16).rearrange("p (b t m) -> p b m t", b=2, t=PACK),
+            wx_raw[:].bitcast(U16).rearrange("p (b m t) -> p b m t", b=2, t=PACK),
+        )
+        nc.vector.tensor_copy(
+            wx_plane[:].rearrange("p (b t m) -> p b m t", b=2, t=PACK),
+            wx_plane_raw[:].bitcast(U8).rearrange("p (b m t) -> p b m t", b=2, t=PACK),
+        )
+
+        w1_bf = {}
+        w1_codes = {}
+        w1_plane = {}
+        for a in range(2):
+            for b in range(2):
+                w1_codes[a, b] = held("w1_codes%d%d" % (a, b), [P, KP], U32)
+                w1_plane[a, b] = held("w1_plane%d%d" % (a, b), [P, KP], U8)
+
+        def negate_on_scalar(dst, src):
+            nc.scalar.activation(dst, src, ACT.Copy, scale=-1.0)
+
+        def negate_on_vector(dst, src):
+            nc.vector.tensor_scalar(dst, src, -1.0, None, ALU.mult)
+
+        def round_w1(copy, a, b, raw, m0):
+            width = raw.shape[2] // PACK
+            if m0 == 0:
+                w1_bf[a, b] = work.tile([P, PACK * KP], BF16, name="w1_bf", bufs=2, align_bytes=64)
+            dst = w1_bf[a, b][:].rearrange("p (t m i) -> p m i t", t=PACK, i=PACK)[:, m0 : m0 + width]
+            copy(dst, raw[:].rearrange("p i (m t) -> p m i t", t=PACK))
+
+        def quantise_w1(a, b):
+            nc.vector.quantize_mx(w1_codes[a, b][:].bitcast(FP8X4), w1_plane[a, b][:], w1_bf[a, b][:])
+
+        round_w1(negate_on_scalar, 0, 0, w1_00, 0)
+        quantise_w1(0, 0)
+
+        def beam_pass(bank, b, jc, t, stop):
+            c0 = b * KP + t * P
+            nc.tensor.matmul_mx(
+                bank[:],
+                lhsT=wx_codes[:, 2 * c0 : 2 * (c0 + P)].bitcast(FP4X4),
+                lhsT_scale=wx_plane[:, c0 : c0 + P],
+                rhs=xs_codes[:, jc * JC : (jc + 1) * JC].bitcast(FP8X4),
+                rhs_scale=xs_plane[:].bitcast(U8)[:, jc * JC : (jc + 1) * JC],
+                start=True,
+                stop=stop,
+            )
+
+        gained_beam = {}
+        for b in range(2):
+            for jc in range(2):
+                for t in range(PACK):
+                    bank = psum.tile([P, JC], F32, name="single", bufs=3)
+                    beam_pass(bank, b, jc, t, True)
+                    gb = held("gb%d%d%d" % (b, jc, t), [P, JC], F32)
+                    nc.scalar.activation(gb[:], bank[:], ACT.Copy, scale=gains[:, b, t : t + 1])
+                    gained_beam[b, jc, t] = gb
+
+        v_planes = held("v_planes", [P, S], U8)
+        nc.vector.tensor_copy(v_planes[:], tab_planes[:].bitcast(U8).indirect(offsets[:]))
+        v_codes = {}
+        for a in range(2):
+            for jc in range(2):
+                v_codes[a, jc] = held("v_codes%d%d" % (a, jc), [P, JC], U32)
+                piece = offsets[:, jc * (JC // 16) : (jc + 1) * (JC // 16)]
+                nc.vector.tensor_copy(v_codes[a, jc][:], tab[a][:].bitcast(U32).indirect(piece))
+
+        round_w1(negate_on_scalar, 1, 0, w1_10a, 0)
+        round_w1(negate_on_vector, 1, 0, w1_10b, P // 2)
+        quantise_w1(1, 0)
+
+        w3_bf = held("w3_bf", [P, 2 * N * PACK], BF16)
+        w3_codes = held("w3_codes", [P, 2 * N], U32)
+        w3_plane = held("w3_plane", [P, 2 * N], U8)
+        h_codes = [held("h_codes%d" % b, [P, S], U32) for b in range(2)]
+        h_plane = [held("h_plane%d" % b, [P, S], U8) for b in range(2)]
+
+        def round_w3(copy, a):
+            dst = w3_bf[:, a * N * PACK : (a + 1) * N * PACK].rearrange("p (c e i) -> p c i e", e=4, i=PACK)
+            copy(dst, w3_raw[a][:].rearrange("p i (c e) -> p c i e", e=4))
+
+        def quantise_w3(w0, w_end):
+            nc.vector.quantize_mx(
+                w3_codes[:, w0:w_end].bitcast(FP8X4), w3_plane[:, w0:w_end], w3_bf[:, PACK * w0 : PACK * w_end]
+            )
+
+        banks = {}
+        deps = {}
+        rows = {}
+
+        def in_psum(b, jc, t):
+            return 8 * b + 4 * jc + t >= 16 - REPEATS
+
+        def products(b, jc, t):
+            bank = psum.tile([P, JC], F32, name="prof", bufs=5)
+            banks[b, jc, t] = bank
+            cols = slice(t * P, (t + 1) * P)
+            if in_psum(b, jc, t):
+                beam_pass(bank, b, jc, t, False)
+            for a in range(2):
+                nc.tensor.matmul_mx(
+                    bank[:],
+                    lhsT=w1_codes[a, b][:, cols].bitcast(FP8X4),
+                    lhsT_scale=w1_plane[a, b][:, cols],
+                    rhs=v_codes[a, jc][:].bitcast(FP8X4),
+                    rhs_scale=v_planes[4 * a : P, jc * JC : (jc + 1) * JC],
+                    start=(a == 0 and not in_psum(b, jc, t)),
+                    stop=(a == 1),
+                )
+
+        def squared(b, j0, width, t):
+            jc = j0 // JC
+            cols = slice(j0 - jc * JC, j0 - jc * JC + width)
+            if cols.start == 0:
+                products(b, jc, t)
+            dep = work.tile([P, width], F32, name="dep", bufs=10)
+            deps[b, j0, t] = dep
+            source = banks[b, jc, t][:, cols]
+            if not in_psum(b, jc, t):
+                col = b * PACK + t
+                nc.vector.scalar_tensor_tensor(
+                    dep[:], gained_beam[b, jc, t][:, cols], inv_gains[:, col : col + 1], source, ALU.mult, ALU.add
+                )
+                source = dep[:]
+            nc.scalar.activation(dep[:], source, ACT.Square, bias=biases[:, b, t : t + 1], scale=-1.0)
+
+        def rooted(b, j0, width, t):
+            nc.scalar.activation(deps[b, j0, t][:], deps[b, j0, t][:], ACT.Sqrt, bias=1.0)
+
+        def gained(b, j0, width, t):
+            jc = j0 // JC
+            cols = slice(j0 - jc * JC, j0 - jc * JC + width)
+            if t == 0:
+                rows[b, j0] = work.tile([P, PACK, width], BF16, name="h_rows", bufs=2, align_bytes=64)
+            nc.vector.scalar_tensor_tensor(
+                rows[b, j0][:, t, :],
+                deps[b, j0, t][:],
+                gains[:, b, t : t + 1],
+                gained_beam[b, jc, t][:, cols],
+                ALU.mult,
+                ALU.add,
+            )
+            if t < PACK - 1:
+                return
+            woven = work.tile([P, width * PACK], BF16, name="h_woven", bufs=2, align_bytes=64)
+            nc.vector.tensor_copy(
+                woven[:].rearrange("p (c i t) -> p c t i", i=4, t=PACK),
+                rows[b, j0][:].rearrange("p t (c i) -> p c t i", i=4),
+            )
+            span = slice(j0, j0 + width)
+            nc.vector.quantize_mx(h_codes[b][:, span].bitcast(FP8X4), h_plane[b][:, span], woven[:])
+            if b == 1:
+                scores(j0, width)
+
+        def scores(j0, width):
+            span = slice(j0, j0 + width)
+            for nt in range(N // P):
+                bank = psum.tile([P, width], F32, name="single", bufs=3)
+                for a in range(2):
+                    cols = slice(a * N + nt * P, a * N + (nt + 1) * P)
+                    nc.tensor.matmul_mx(
+                        bank[:],
+                        lhsT=w3_codes[:, cols].bitcast(FP8X4),
+                        lhsT_scale=w3_plane[:, cols],
+                        rhs=h_codes[a][:, span].bitcast(FP8X4),
+                        rhs_scale=h_plane[a][:, span],
+                        start=(a == 0),
+                        stop=(a == 1),
+                    )
+                result = work.tile([P, width], F32, name="result", bufs=6)
+                if j0 + width == S and nt == 1:
+                    nc.vector.tensor_copy(result[:], bank[:])
+                else:
+                    nc.scalar.copy(result[:], bank[:])
+                nc.sync.dma_start(out[nt * P : (nt + 1) * P, span], result[:])
+
+        def weights_of_second_half(a):
+            round_w1(negate_on_scalar, a, 1, w1_second[a], 0)
+            quantise_w1(a, 1)
+
+        def weights_of_scores():
+            round_w3(nc.vector.tensor_copy, 0)
+            round_w3(nc.vector.tensor_copy, 1)
+            quantise_w3(0, 512)
+            quantise_w3(512, 768)
+
+        w1_second = [w1_01, w1_11]
+        spans = [(0, 0, 512), (0, 512, 512), (1, 0, 512), (1, 512, 256), (1, 768, 256)]
+        units = [(b, j0, width, t) for b, j0, width in spans for t in range(PACK)]
+        for n in range(len(units) + 2):
+            if n < len(units):
+                squared(*units[n])
+            if 1 <= n <= len(units):
+                rooted(*units[n - 1])
+            if n >= 2:
+                gained(*units[n - 2])
+            if n == 3:
+                weights_of_second_half(0)
+            if n == 5:
+                weights_of_second_half(1)
+            if n == 6:
+                weights_of_scores()

@@ -65,23 +65,23 @@ def tile_list_toll_axle_scores_kernel(
             nc.sync.dma_start(raw[:], w3[a * KP : (a + 1) * KP, :].rearrange("(p i) n -> p i n", i=PACK))
             return raw
 
-        nc.sync.dma_start(wx_raw[:], wx_words[0].bitcast(I32))
+        nc.gpsimd.dma_start(gains[:], gain.rearrange("(b p t) -> p b t", b=2, t=PACK))
+        nc.gpsimd.dma_start(biases[:], b1.rearrange("(b p t) -> p b t", b=2, t=PACK))
         for q in range(4):
-            nc.sync.dma_start(wx_plane_raw[32 * q : 32 * q + 4, :], wx_scales[0, 4 * q : 4 * q + 4, :].bitcast(I32))
-        w1_00 = load_w1(0, 0, 0, KP, "w1_00")
-        nc.sync.dma_start(xs_codes[:], xs_words[0].rearrange("p n t -> p (n t)").bitcast(I32))
-        nc.sync.dma_start(gains[:], gain.rearrange("(b p t) -> p b t", b=2, t=PACK))
-        for q in range(4):
-            nc.sync.dma_start(xs_plane[32 * q : 32 * q + 4, :], xs_scales[0, 4 * q : 4 * q + 4, :].bitcast(I32))
-        nc.sync.dma_start(offsets[:], offs)
-        nc.sync.dma_start(tab[0][:], tab_words[0].rearrange("p n t -> p (n t)").bitcast(I32))
-        for q in range(4):
-            nc.sync.dma_start(
+            nc.gpsimd.dma_start(
                 tab_planes[32 * q : 32 * q + 8, :],
                 tab_scales[:, 4 * q : 4 * q + 4, :].bitcast(I32),
             )
+        nc.sync.dma_start(wx_raw[:], wx_words[0].bitcast(I32))
+        for q in range(4):
+            nc.sync.dma_start(wx_plane_raw[32 * q : 32 * q + 4, :], wx_scales[0, 4 * q : 4 * q + 4, :].bitcast(I32))
+        nc.sync.dma_start(xs_codes[:], xs_words[0].rearrange("p n t -> p (n t)").bitcast(I32))
+        w1_00 = load_w1(0, 0, 0, KP, "w1_00")
+        nc.sync.dma_start(tab[0][:], tab_words[0].rearrange("p n t -> p (n t)").bitcast(I32))
+        for q in range(4):
+            nc.scalar.dma_start(xs_plane[32 * q : 32 * q + 4, :], xs_scales[0, 4 * q : 4 * q + 4, :].bitcast(I32))
+        nc.sync.dma_start(offsets[:], offs)
         nc.sync.dma_start(tab[1][:], tab_words[1].rearrange("p n t -> p (n t)").bitcast(I32))
-        nc.sync.dma_start(biases[:], b1.rearrange("(b p t) -> p b t", b=2, t=PACK))
         w1_10a = load_w1(1, 0, 0, KP // 2, "w1_10a")
         w1_10b = load_w1(1, 0, KP // 2, KP, "w1_10b")
         w1_01 = load_w1(0, 1, 0, KP, "w1_01")
@@ -159,7 +159,9 @@ def tile_list_toll_axle_scores_kernel(
                     gained_beam[b, jc, t] = gb
 
         v_planes = held("v_planes", [P, S], U8)
-        nc.vector.tensor_copy(v_planes[:], tab_planes[:].bitcast(U8).indirect(offsets[:]))
+        for jc in range(2):
+            piece = offsets[:, jc * (JC // 16) : (jc + 1) * (JC // 16)]
+            nc.vector.tensor_copy(v_planes[:, jc * JC : (jc + 1) * JC], tab_planes[:].bitcast(U8).indirect(piece))
         v_codes = {}
         for a in range(2):
             for jc in range(2):
@@ -169,7 +171,11 @@ def tile_list_toll_axle_scores_kernel(
 
         round_w1(negate_on_scalar, 1, 0, w1_10a, 0)
         round_w1(negate_on_vector, 1, 0, w1_10b, P // 2)
-        quantise_w1(1, 0)
+        for t in range(PACK):
+            cols = slice(t * P, (t + 1) * P)
+            nc.vector.quantize_mx(
+                w1_codes[1, 0][:, cols].bitcast(FP8X4), w1_plane[1, 0][:, cols], w1_bf[1, 0][:, t * KP : (t + 1) * KP]
+            )
 
         w3_bf = held("w3_bf", [P, 2 * N * PACK], BF16)
         w3_codes = held("w3_codes", [P, 2 * N], U32)

@@ -43,8 +43,8 @@ def tile_list_toll_axle_scores_kernel(
         xs_plane = held("xs_plane", [P, S // 4], I32)
         tab_planes = held("tab_planes", [P, T // 4], I32)
         tab = [held("tab%d" % a, [P, T], I32) for a in range(2)]
-        gains = held("gains", [P, 2, PACK], F32)
-        biases = held("biases", [P, 2, PACK], F32)
+        gains = held("gains", [P, 2, 8], F32)
+        biases = held("biases", [P, 2, 8], F32)
         warm = held("warm", [P, 1], F32)
         warm_out = held("warm_out", [P, 1], F32)
 
@@ -65,34 +65,40 @@ def tile_list_toll_axle_scores_kernel(
             nc.sync.dma_start(raw[:], w3[a * KP : (a + 1) * KP, :].rearrange("(p i) n -> p i n", i=PACK))
             return raw
 
-        nc.gpsimd.dma_start(gains[:], gain.rearrange("(b p t) -> p b t", b=2, t=PACK))
-        nc.gpsimd.dma_start(biases[:], b1.rearrange("(b p t) -> p b t", b=2, t=PACK))
-        for q in range(4):
-            nc.gpsimd.dma_start(
-                tab_planes[32 * q : 32 * q + 8, :],
-                tab_scales[:, 4 * q : 4 * q + 4, :].bitcast(I32),
-            )
+        def load_plane(plane, first, scales, r):
+            nc.sync.dma_start(plane[first + r : P : 32, :], scales[r:16:4, :].bitcast(I32))
+
+        def load_channels(tile, vector):
+            nc.sync.dma_start(tile[:, :, 0:PACK], vector.rearrange("(b p t) -> p b t", b=2, t=PACK))
+
+        def load_table(a, c0, c1):
+            nc.sync.dma_start(tab[a][:, c0:c1], tab_words[a].rearrange("p n t -> p (n t)").bitcast(I32)[:, c0:c1])
+
+        load_channels(gains, gain)
         nc.sync.dma_start(wx_raw[:], wx_words[0].bitcast(I32))
-        for q in range(4):
-            nc.sync.dma_start(wx_plane_raw[32 * q : 32 * q + 4, :], wx_scales[0, 4 * q : 4 * q + 4, :].bitcast(I32))
         nc.sync.dma_start(xs_codes[:], xs_words[0].rearrange("p n t -> p (n t)").bitcast(I32))
+        for r in range(4):
+            load_plane(wx_plane_raw, 0, wx_scales[0], r)
         w1_00 = load_w1(0, 0, 0, KP, "w1_00")
-        nc.sync.dma_start(tab[0][:], tab_words[0].rearrange("p n t -> p (n t)").bitcast(I32))
-        for q in range(4):
-            nc.scalar.dma_start(xs_plane[32 * q : 32 * q + 4, :], xs_scales[0, 4 * q : 4 * q + 4, :].bitcast(I32))
+        for r in range(4):
+            load_plane(xs_plane, 0, xs_scales[0], r)
         nc.sync.dma_start(offsets[:], offs)
-        nc.sync.dma_start(tab[1][:], tab_words[1].rearrange("p n t -> p (n t)").bitcast(I32))
-        w1_10a = load_w1(1, 0, 0, KP // 2, "w1_10a")
-        w1_10b = load_w1(1, 0, KP // 2, KP, "w1_10b")
+        for a in range(2):
+            load_table(0, a * T // 2, (a + 1) * T // 2)
+            for r in range(4):
+                load_plane(tab_planes, 4 * a + 4, tab_scales[a], r)
+        load_table(1, 0, T)
+        w1_10 = load_w1(1, 0, 0, KP, "w1_10")
+        load_channels(biases, b1)
         w1_01 = load_w1(0, 1, 0, KP, "w1_01")
         w1_11 = load_w1(1, 1, 0, KP, "w1_11")
         w3_raw = [load_w3(a) for a in range(2)]
 
-        flat_gains = gains[:].rearrange("p b t -> p (b t)")
-        neg_gains = held("neg_gains", [P, 8], F32)
-        abs_gains = held("abs_gains", [P, 8], F32)
-        denom = held("denom", [P, 8], F32)
-        inv_gains = held("inv_gains", [P, 8], F32)
+        flat_gains = gains[:, :, 0:PACK]
+        neg_gains = held("neg_gains", [P, 2, PACK], F32)
+        abs_gains = held("abs_gains", [P, 2, PACK], F32)
+        denom = held("denom", [P, 2, PACK], F32)
+        inv_gains = held("inv_gains", [P, 2, PACK], F32)
         nc.vector.tensor_scalar(neg_gains[:], flat_gains, -1.0, None, ALU.mult)
         nc.vector.tensor_tensor(abs_gains[:], neg_gains[:], flat_gains, ALU.max)
         nc.vector.scalar_tensor_tensor(denom[:], abs_gains[:], TINY, flat_gains, ALU.is_lt, ALU.add)
@@ -123,17 +129,16 @@ def tile_list_toll_axle_scores_kernel(
         def negate_on_vector(dst, src):
             nc.vector.tensor_scalar(dst, src, -1.0, None, ALU.mult)
 
-        def round_w1(copy, a, b, raw, m0):
-            width = raw.shape[2] // PACK
+        def round_w1(copy, a, b, raw, m0, m1):
             if m0 == 0:
                 w1_bf[a, b] = work.tile([P, PACK * KP], BF16, name="w1_bf", bufs=2, align_bytes=64)
-            dst = w1_bf[a, b][:].rearrange("p (t m i) -> p m i t", t=PACK, i=PACK)[:, m0 : m0 + width]
-            copy(dst, raw[:].rearrange("p i (m t) -> p m i t", t=PACK))
+            dst = w1_bf[a, b][:].rearrange("p (t m i) -> p m i t", t=PACK, i=PACK)[:, m0:m1]
+            copy(dst, raw[:].rearrange("p i (m t) -> p m i t", t=PACK)[:, m0:m1])
 
         def quantise_w1(a, b):
             nc.vector.quantize_mx(w1_codes[a, b][:].bitcast(FP8X4), w1_plane[a, b][:], w1_bf[a, b][:])
 
-        round_w1(negate_on_scalar, 0, 0, w1_00, 0)
+        round_w1(negate_on_vector, 0, 0, w1_00, 0, P)
         quantise_w1(0, 0)
 
         def beam_pass(bank, b, jc, t, stop):
@@ -169,8 +174,8 @@ def tile_list_toll_axle_scores_kernel(
                 piece = offsets[:, jc * (JC // 16) : (jc + 1) * (JC // 16)]
                 nc.vector.tensor_copy(v_codes[a, jc][:], tab[a][:].bitcast(U32).indirect(piece))
 
-        round_w1(negate_on_scalar, 1, 0, w1_10a, 0)
-        round_w1(negate_on_vector, 1, 0, w1_10b, P // 2)
+        round_w1(negate_on_scalar, 1, 0, w1_10, 0, 40)
+        round_w1(negate_on_vector, 1, 0, w1_10, 40, P)
         for t in range(PACK):
             cols = slice(t * P, (t + 1) * P)
             nc.vector.quantize_mx(
@@ -195,6 +200,7 @@ def tile_list_toll_axle_scores_kernel(
         banks = {}
         deps = {}
         rows = {}
+        wovens = {}
 
         def in_psum(b, jc, t):
             return 8 * b + 4 * jc + t >= 16 - REPEATS
@@ -211,7 +217,7 @@ def tile_list_toll_axle_scores_kernel(
                     lhsT=w1_codes[a, b][:, cols].bitcast(FP8X4),
                     lhsT_scale=w1_plane[a, b][:, cols],
                     rhs=v_codes[a, jc][:].bitcast(FP8X4),
-                    rhs_scale=v_planes[4 * a : P, jc * JC : (jc + 1) * JC],
+                    rhs_scale=v_planes[4 * a + 4 : P, jc * JC : (jc + 1) * JC],
                     start=(a == 0 and not in_psum(b, jc, t)),
                     stop=(a == 1),
                 )
@@ -225,9 +231,8 @@ def tile_list_toll_axle_scores_kernel(
             deps[b, j0, t] = dep
             source = banks[b, jc, t][:, cols]
             if not in_psum(b, jc, t):
-                col = b * PACK + t
                 nc.vector.scalar_tensor_tensor(
-                    dep[:], gained_beam[b, jc, t][:, cols], inv_gains[:, col : col + 1], source, ALU.mult, ALU.add
+                    dep[:], gained_beam[b, jc, t][:, cols], inv_gains[:, b, t : t + 1], source, ALU.mult, ALU.add
                 )
                 source = dep[:]
             nc.scalar.activation(dep[:], source, ACT.Square, bias=biases[:, b, t : t + 1], scale=-1.0)
@@ -248,15 +253,18 @@ def tile_list_toll_axle_scores_kernel(
                 ALU.mult,
                 ALU.add,
             )
-            if t < PACK - 1:
-                return
+
+        def weave(b, j0, width):
             woven = work.tile([P, width * PACK], BF16, name="h_woven", bufs=2, align_bytes=64)
             nc.vector.tensor_copy(
                 woven[:].rearrange("p (c i t) -> p c t i", i=4, t=PACK),
                 rows[b, j0][:].rearrange("p t (c i) -> p c t i", i=4),
             )
+            wovens[b, j0] = woven
+
+        def quantise_h(b, j0, width):
             span = slice(j0, j0 + width)
-            nc.vector.quantize_mx(h_codes[b][:, span].bitcast(FP8X4), h_plane[b][:, span], woven[:])
+            nc.vector.quantize_mx(h_codes[b][:, span].bitcast(FP8X4), h_plane[b][:, span], wovens[b, j0][:])
             if b == 1:
                 scores(j0, width)
 
@@ -283,7 +291,7 @@ def tile_list_toll_axle_scores_kernel(
                 nc.sync.dma_start(out[nt * P : (nt + 1) * P, span], result[:])
 
         def weights_of_second_half(a):
-            round_w1(negate_on_scalar, a, 1, w1_second[a], 0)
+            round_w1(negate_on_scalar, a, 1, w1_second[a], 0, P)
             quantise_w1(a, 1)
 
         def weights_of_scores():
@@ -295,13 +303,17 @@ def tile_list_toll_axle_scores_kernel(
         w1_second = [w1_01, w1_11]
         spans = [(0, 0, 512), (0, 512, 512), (1, 0, 512), (1, 512, 256), (1, 768, 256)]
         units = [(b, j0, width, t) for b, j0, width in spans for t in range(PACK)]
-        for n in range(len(units) + 2):
+        for n in range(len(units) + 4):
             if n < len(units):
                 squared(*units[n])
             if 1 <= n <= len(units):
                 rooted(*units[n - 1])
-            if n >= 2:
+            if 2 <= n < len(units) + 2:
                 gained(*units[n - 2])
+            if n >= 3 and (n - 3) % PACK == PACK - 1:
+                weave(*spans[(n - 3) // PACK])
+            if n >= 4 and (n - 4) % PACK == PACK - 1:
+                quantise_h(*spans[(n - 4) // PACK])
             if n == 3:
                 weights_of_second_half(0)
             if n == 5:

from contextlib import ExitStack

import concourse.mybir as mybir

K, K2, H, N, T, S = 1024, 512, 1024, 384, 4096, 1024
FLOPS = 2 * (K * H * S + K2 * H * S + H * N * S)

F32 = mybir.dt.float32
BF16 = mybir.dt.bfloat16
I32 = mybir.dt.int32
U32 = mybir.dt.uint32
U16 = mybir.dt.uint16
U8 = mybir.dt.uint8
FP8X4 = mybir.dt.float8_e4m3fn_x4
FP4X4 = mybir.dt.float4_e2m1fn_x4
ALU = mybir.AluOpType
ACT = mybir.ActivationFunctionType

P = 128
PACK = 4
KP = P * PACK
JC = 512
TINY = 2.0 ** -120
REPEATS = 6


def tile_list_toll_axle_scores_kernel(
    tc, tab_words, tab_scales, offs, xs_words, xs_scales, w1, wx_words, wx_scales, b1, gain, w3, out
):
    nc = tc.nc
    with ExitStack() as ctx:
        keep = ctx.enter_context(tc.tile_pool(name="keep", bufs=1))
        work = ctx.enter_context(tc.tile_pool(name="work", bufs=4))
        psum = ctx.enter_context(tc.psum_pool(name="psum", bufs=1))

        def held(name, shape, dtype):
            return keep.tile(shape, dtype, name=name, align_bytes=64)

        offsets = keep.tile([P, S // 16], U16, name="offsets")
        wx_raw = held("wx_raw", [P, H // 2], I32)
        wx_plane_raw = held("wx_plane_raw", [P, H // 4], I32)
        xs_codes = held("xs_codes", [P, S], I32)
        xs_plane = held("xs_plane", [P, S // 4], I32)
        tab_planes = held("tab_planes", [P, T // 4], I32)
        tab = [held("tab%d" % a, [P, T], I32) for a in range(2)]
        gains = held("gains", [P, 2, 8], F32)
        biases = held("biases", [P, 2, 8], F32)
        warm = held("warm", [P, 1], F32)
        warm_out = held("warm_out", [P, 1], F32)

        nc.vector.memset(wx_plane_raw[:], 0)
        nc.vector.memset(xs_plane[:], 0)
        nc.vector.memset(tab_planes[:], 0)
        nc.vector.memset(warm[:], 1.0)
        nc.scalar.activation(warm_out[:], warm[:], ACT.Sqrt)

        def load_w1(a, b, c0, c1, name):
            raw = held(name, [P, PACK, c1 - c0], F32)
            rows = w1[a * KP : (a + 1) * KP, b * KP + c0 : b * KP + c1]
            nc.sync.dma_start(raw[:], rows.rearrange("(p i) c -> p i c", i=PACK))
            return raw

        def load_w3(a):
            raw = held("w3_raw%d" % a, [P, PACK, N], F32)
            nc.sync.dma_start(raw[:], w3[a * KP : (a + 1) * KP, :].rearrange("(p i) n -> p i n", i=PACK))
            return raw

        def load_plane(plane, first, scales, r):
            nc.sync.dma_start(plane[first + r : P : 32, :], scales[r:16:4, :].bitcast(I32))

        def load_channels(tile, vector):
            nc.sync.dma_start(tile[:, :, 0:PACK], vector.rearrange("(b p t) -> p b t", b=2, t=PACK))

        def load_table(a, c0, c1):
            nc.sync.dma_start(tab[a][:, c0:c1], tab_words[a].rearrange("p n t -> p (n t)").bitcast(I32)[:, c0:c1])

        load_channels(gains, gain)
        nc.sync.dma_start(wx_raw[:], wx_words[0].bitcast(I32))
        nc.sync.dma_start(xs_codes[:], xs_words[0].rearrange("p n t -> p (n t)").bitcast(I32))
        for r in range(4):
            load_plane(wx_plane_raw, 0, wx_scales[0], r)
        w1_00 = load_w1(0, 0, 0, KP, "w1_00")
        for r in range(4):
            load_plane(xs_plane, 0, xs_scales[0], r)
        nc.sync.dma_start(offsets[:], offs)
        for a in range(2):
            load_table(0, a * T // 2, (a + 1) * T // 2)
            for r in range(4):
                load_plane(tab_planes, 4 * a + 4, tab_scales[a], r)
        load_table(1, 0, T)
        w1_10 = load_w1(1, 0, 0, KP, "w1_10")
        load_channels(biases, b1)
        w1_01 = load_w1(0, 1, 0, KP, "w1_01")
        w1_11 = load_w1(1, 1, 0, KP, "w1_11")
        w3_raw = [load_w3(a) for a in range(2)]

        flat_gains = gains[:, :, 0:PACK]
        neg_gains = held("neg_gains", [P, 2, PACK], F32)
        abs_gains = held("abs_gains", [P, 2, PACK], F32)
        denom = held("denom", [P, 2, PACK], F32)
        inv_gains = held("inv_gains", [P, 2, PACK], F32)
        nc.vector.tensor_scalar(neg_gains[:], flat_gains, -1.0, None, ALU.mult)
        nc.vector.tensor_tensor(abs_gains[:], neg_gains[:], flat_gains, ALU.max)
        nc.vector.scalar_tensor_tensor(denom[:], abs_gains[:], TINY, flat_gains, ALU.is_lt, ALU.add)
        nc.vector.reciprocal(inv_gains[:], denom[:])

        wx_codes = held("wx_codes", [P, 2 * H], U8)
        wx_plane = held("wx_plane", [P, H], U8)
        nc.vector.tensor_copy(
            wx_codes[:].bitcast(U16).rearrange("p (b t m) -> p b m t", b=2, t=PACK),
            wx_raw[:].bitcast(U16).rearrange("p (b m t) -> p b m t", b=2, t=PACK),
        )
        nc.vector.tensor_copy(
            wx_plane[:].rearrange("p (b t m) -> p b m t", b=2, t=PACK),
            wx_plane_raw[:].bitcast(U8).rearrange("p (b m t) -> p b m t", b=2, t=PACK),
        )

        w1_bf = {}
        w1_codes = {}
        w1_plane = {}
        for a in range(2):
            for b in range(2):
                w1_codes[a, b] = held("w1_codes%d%d" % (a, b), [P, KP], U32)
                w1_plane[a, b] = held("w1_plane%d%d" % (a, b), [P, KP], U8)

        def negate_on_scalar(dst, src):
            nc.scalar.activation(dst, src, ACT.Copy, scale=-1.0)

        def negate_on_vector(dst, src):
            nc.vector.tensor_scalar(dst, src, -1.0, None, ALU.mult)

        def round_w1(copy, a, b, raw, m0, m1):
            if m0 == 0:
                w1_bf[a, b] = work.tile([P, PACK * KP], BF16, name="w1_bf", bufs=2, align_bytes=64)
            dst = w1_bf[a, b][:].rearrange("p (t m i) -> p m i t", t=PACK, i=PACK)[:, m0:m1]
            copy(dst, raw[:].rearrange("p i (m t) -> p m i t", t=PACK)[:, m0:m1])

        def quantise_w1(a, b):
            nc.vector.quantize_mx(w1_codes[a, b][:].bitcast(FP8X4), w1_plane[a, b][:], w1_bf[a, b][:])

        round_w1(negate_on_vector, 0, 0, w1_00, 0, P)
        quantise_w1(0, 0)

        def beam_pass(bank, b, jc, t, stop):
            c0 = b * KP + t * P
            nc.tensor.matmul_mx(
                bank[:],
                lhsT=wx_codes[:, 2 * c0 : 2 * (c0 + P)].bitcast(FP4X4),
                lhsT_scale=wx_plane[:, c0 : c0 + P],
                rhs=xs_codes[:, jc * JC : (jc + 1) * JC].bitcast(FP8X4),
                rhs_scale=xs_plane[:].bitcast(U8)[:, jc * JC : (jc + 1) * JC],
                start=True,
                stop=stop,
            )

        gained_beam = {}
        for b in range(2):
            for jc in range(2):
                for t in range(PACK):
                    bank = psum.tile([P, JC], F32, name="single", bufs=3)
                    beam_pass(bank, b, jc, t, True)
                    gb = held("gb%d%d%d" % (b, jc, t), [P, JC], F32)
                    nc.scalar.activation(gb[:], bank[:], ACT.Copy, scale=gains[:, b, t : t + 1])
                    gained_beam[b, jc, t] = gb

        v_planes = held("v_planes", [P, S], U8)
        for jc in range(2):
            piece = offsets[:, jc * (JC // 16) : (jc + 1) * (JC // 16)]
            nc.vector.tensor_copy(v_planes[:, jc * JC : (jc + 1) * JC], tab_planes[:].bitcast(U8).indirect(piece))
        v_codes = {}
        for a in range(2):
            for jc in range(2):
                v_codes[a, jc] = held("v_codes%d%d" % (a, jc), [P, JC], U32)
                piece = offsets[:, jc * (JC // 16) : (jc + 1) * (JC // 16)]
                nc.vector.tensor_copy(v_codes[a, jc][:], tab[a][:].bitcast(U32).indirect(piece))

        round_w1(negate_on_scalar, 1, 0, w1_10, 0, 40)
        round_w1(negate_on_vector, 1, 0, w1_10, 40, P)
        for t in range(PACK):
            cols = slice(t * P, (t + 1) * P)
            nc.vector.quantize_mx(
                w1_codes[1, 0][:, cols].bitcast(FP8X4), w1_plane[1, 0][:, cols], w1_bf[1, 0][:, t * KP : (t + 1) * KP]
            )

        w3_bf = held("w3_bf", [P, 2 * N * PACK], BF16)
        w3_codes = held("w3_codes", [P, 2 * N], U32)
        w3_plane = held("w3_plane", [P, 2 * N], U8)
        h_codes = [held("h_codes%d" % b, [P, S], U32) for b in range(2)]
        h_plane = [held("h_plane%d" % b, [P, S], U8) for b in range(2)]

        def round_w3(copy, a):
            dst = w3_bf[:, a * N * PACK : (a + 1) * N * PACK].rearrange("p (c e i) -> p c i e", e=4, i=PACK)
            copy(dst, w3_raw[a][:].rearrange("p i (c e) -> p c i e", e=4))

        def quantise_w3(w0, w_end):
            nc.vector.quantize_mx(
                w3_codes[:, w0:w_end].bitcast(FP8X4), w3_plane[:, w0:w_end], w3_bf[:, PACK * w0 : PACK * w_end]
            )

        banks = {}
        deps = {}
        rows = {}
        wovens = {}

        def in_psum(b, jc, t):
            return 8 * b + 4 * jc + t >= 16 - REPEATS

        def products(b, jc, t):
            bank = psum.tile([P, JC], F32, name="prof", bufs=5)
            banks[b, jc, t] = bank
            cols = slice(t * P, (t + 1) * P)
            if in_psum(b, jc, t):
                beam_pass(bank, b, jc, t, False)
            for a in range(2):
                nc.tensor.matmul_mx(
                    bank[:],
                    lhsT=w1_codes[a, b][:, cols].bitcast(FP8X4),
                    lhsT_scale=w1_plane[a, b][:, cols],
                    rhs=v_codes[a, jc][:].bitcast(FP8X4),
                    rhs_scale=v_planes[4 * a + 4 : P, jc * JC : (jc + 1) * JC],
                    start=(a == 0 and not in_psum(b, jc, t)),
                    stop=(a == 1),
                )

        def squared(b, j0, width, t):
            jc = j0 // JC
            cols = slice(j0 - jc * JC, j0 - jc * JC + width)
            if cols.start == 0:
                products(b, jc, t)
            dep = work.tile([P, width], F32, name="dep", bufs=10)
            deps[b, j0, t] = dep
            source = banks[b, jc, t][:, cols]
            if not in_psum(b, jc, t):
                nc.vector.scalar_tensor_tensor(
                    dep[:], gained_beam[b, jc, t][:, cols], inv_gains[:, b, t : t + 1], source, ALU.mult, ALU.add
                )
                source = dep[:]
            nc.scalar.activation(dep[:], source, ACT.Square, bias=biases[:, b, t : t + 1], scale=-1.0)

        def rooted(b, j0, width, t):
            nc.scalar.activation(deps[b, j0, t][:], deps[b, j0, t][:], ACT.Sqrt, bias=1.0)

        def gained(b, j0, width, t):
            jc = j0 // JC
            cols = slice(j0 - jc * JC, j0 - jc * JC + width)
            if t == 0:
                rows[b, j0] = work.tile([P, PACK, width], BF16, name="h_rows", bufs=2, align_bytes=64)
            nc.vector.scalar_tensor_tensor(
                rows[b, j0][:, t, :],
                deps[b, j0, t][:],
                gains[:, b, t : t + 1],
                gained_beam[b, jc, t][:, cols],
                ALU.mult,
                ALU.add,
            )

        def weave(b, j0, width):
            woven = work.tile([P, width * PACK], BF16, name="h_woven", bufs=2, align_bytes=64)
            nc.vector.tensor_copy(
                woven[:].rearrange("p (c i t) -> p c t i", i=4, t=PACK),
                rows[b, j0][:].rearrange("p t (c i) -> p c t i", i=4),
            )
            wovens[b, j0] = woven

        def quantise_h(b, j0, width):
            span = slice(j0, j0 + width)
            nc.vector.quantize_mx(h_codes[b][:, span].bitcast(FP8X4), h_plane[b][:, span], wovens[b, j0][:])
            if b == 1:
                scores(j0, width)

        def scores(j0, width):
            span = slice(j0, j0 + width)
            for nt in range(N // P):
                bank = psum.tile([P, width], F32, name="single", bufs=3)
                for a in range(2):
                    cols = slice(a * N + nt * P, a * N + (nt + 1) * P)
                    nc.tensor.matmul_mx(
                        bank[:],
                        lhsT=w3_codes[:, cols].bitcast(FP8X4),
                        lhsT_scale=w3_plane[:, cols],
                        rhs=h_codes[a][:, span].bitcast(FP8X4),
                        rhs_scale=h_plane[a][:, span],
                        start=(a == 0),
                        stop=(a == 1),
                    )
                result = work.tile([P, width], F32, name="result", bufs=6)
                if j0 + width == S and nt == 1:
                    nc.vector.tensor_copy(result[:], bank[:])
                else:
                    nc.scalar.copy(result[:], bank[:])
                nc.sync.dma_start(out[nt * P : (nt + 1) * P, span], result[:])

        def weights_of_second_half(a):
            round_w1(negate_on_scalar, a, 1, w1_second[a], 0, P)
            quantise_w1(a, 1)

        def weights_of_scores():
            round_w3(nc.vector.tensor_copy, 0)
            round_w3(nc.vector.tensor_copy, 1)
            quantise_w3(0, 512)
            quantise_w3(512, 768)

        w1_second = [w1_01, w1_11]
        spans = [(0, 0, 512), (0, 512, 512), (1, 0, 512), (1, 512, 256), (1, 768, 256)]
        units = [(b, j0, width, t) for b, j0, width in spans for t in range(PACK)]
        for n in range(len(units) + 4):
            if n < len(units):
                squared(*units[n])
            if 1 <= n <= len(units):
                rooted(*units[n - 1])
            if 2 <= n < len(units) + 2:
                gained(*units[n - 2])
            if n >= 3 and (n - 3) % PACK == PACK - 1:
                weave(*spans[(n - 3) // PACK])
            if n >= 4 and (n - 4) % PACK == PACK - 1:
                quantise_h(*spans[(n - 4) // PACK])
            if n == 3:
                weights_of_second_half(0)
            if n == 5:
                weights_of_second_half(1)
            if n == 6:
                weights_of_scores()
